import numpy as np
import ml_dtypes


def mxq(x, axis, fmt="e4m3"):
    dtype, down = {"e4m3": (ml_dtypes.float8_e4m3fn, 7), "e5m2": (ml_dtypes.float8_e5m2, 14)}[fmt]
    v = np.moveaxis(np.asarray(x, np.float32).astype(ml_dtypes.bfloat16).astype(np.float64), axis, -1)
    blocks = v.reshape(v.shape[:-1] + (-1, 32))
    amax = np.abs(blocks).max(-1, keepdims=True)
    byte = np.maximum(np.where(amax > 0, np.frexp(amax)[1] - 1 + 127, 0) - down, 1)
    scale = np.exp2(byte - 127.0)
    codes = (blocks / scale).astype(np.float32).astype(dtype).astype(np.float64)
    return np.moveaxis((codes * scale).reshape(v.shape), -1, axis)


WIDE = False


def mx_kscale(k):
    if not WIDE:
        return np.ones(k)
    levels = np.array([30, -30])
    if k % 512:
        return np.exp2(np.random.permutation(np.resize(levels, k // 32))).repeat(32)
    a = np.empty((k // 512, 16))
    for p in range(k // 512):
        a[p, :8] = np.random.permutation(np.resize(levels, 8))
        for g in range(8):
            far = levels[np.abs(levels - a[p, g]) >= 10]
            a[p, g + 8] = far[np.random.randint(len(far))]
    return np.exp2(a.ravel()).repeat(32)


def f64(x):
    return np.asarray(x).astype(np.float64)


def striped(idx):
    return np.tile(np.asarray(idx).reshape(-1, 16).T, (8, 1)).astype(np.uint16)


def unstriped(offs):
    return offs[:16].T.reshape(-1).astype(np.int64)


E2M1 = np.array([0.0, 0.5, 1.0, 1.5, 2.0, 3.0, 4.0, 6.0, -0.0, -0.5, -1.0, -1.5, -2.0, -3.0, -4.0, -6.0])


def pack_weight(w, fmt):
    k, n = w.shape
    w = f64(np.asarray(w, np.float32).astype(ml_dtypes.bfloat16)).reshape(k // 32, 32, n)
    amax = np.abs(w).max(1)
    if fmt == "e4m3":
        byte = np.frexp(amax)[1] - 1 + 127 - 7
    else:
        mant, ex = np.frexp(amax / 6.0)
        byte = np.where(mant > 0.5, ex, ex - 1) + 127
    byte = np.clip(np.where(amax > 0, byte, 1), 1, 254)
    scaled = (w * np.exp2(127.0 - byte)[:, None, :]).reshape(k, n).astype(np.float32)
    by_word = np.ascontiguousarray(scaled.reshape(k // 512, 128, 4, n).transpose(0, 1, 3, 2))
    if fmt == "e4m3":
        words = by_word.astype(ml_dtypes.float8_e4m3fn).view(np.uint8)
    else:
        c = by_word.astype(ml_dtypes.float4_e2m1fn).view(np.uint8) & 0xF
        words = (c[..., 0::2] | (c[..., 1::2] << 4)).reshape(k // 512, 128, 2 * n)
    return np.ascontiguousarray(words), np.ascontiguousarray(byte.astype(np.uint8).reshape(k // 512, 16, n))


def unpack_weight(words, scales, fmt):
    g, _, n = scales.shape
    words = np.ascontiguousarray(words).reshape(g, 128, n, -1)
    if fmt == "e4m3":
        vals = words.view(ml_dtypes.float8_e4m3fn).astype(np.float64)
    else:
        nib = np.empty((g, 128, n, 4), np.uint8)
        nib[..., 0::2] = words & 0xF
        nib[..., 1::2] = words >> 4
        vals = E2M1[nib]
    vals = vals * np.repeat(np.exp2(scales.astype(np.float64) - 127.0), 8, axis=1)[..., None]
    return vals.transpose(0, 1, 3, 2).reshape(g * 512, n)


K, J, N, R, T, B, V, Q = 512, 512, 256, 256, 1024, 64, 1024, 1024


def setup_inputs():
    n = np.random.standard_normal
    idx = np.random.permutation(T)[:J]
    idx2 = np.random.permutation(V)[:J]
    idx3 = np.random.permutation(Q)[:N]
    fj = mx_kscale(J)
    fk = mx_kscale(K)
    drp = pack_weight(n((K, R)) * 1 / np.sqrt(K) / fk[:, None], "e4m3")
    return {
        "xf": (n((K, T))).astype(np.float32),
        "ra": (np.random.uniform(0.5, 1.5, (1, J)) * fj).astype(np.float32),
        "gt": (n((N, V)) * np.exp(0.5 * n((1, V)))).astype(np.float32),
        "cb": (np.random.uniform(0.5, 1.5, (J, 1)) / fj[:, None]).astype(np.float32),
        "fkr": (np.random.uniform(0.5, 1.5, (1, K)) * fk).astype(np.float32),
        "dr_words": drp[0],
        "dr_scales": drp[1],
        "old": (0.5 * n((R, Q))).astype(np.float32),
        "offs": striped(idx),
        "offs2": striped(idx2),
        "offs3": striped(idx3),
    }


def reference(xf, ra, gt, cb, fkr, dr_words, dr_scales, old, offs, offs2, offs3):
    idx = unstriped(offs)
    idx2 = unstriped(offs2)
    idx3 = unstriped(offs3)
    dru = unpack_weight(dr_words, dr_scales, "e4m3")
    xg = f64(xf)[:, idx]
    g1 = xg.reshape(K, B, J // B).mean(axis=2)
    g2 = np.repeat(g1, J // B, axis=1)
    us = (xg - g2) * f64(ra)
    ut = us.T
    uj = ut * f64(fkr)
    gr1 = f64(gt)[:, idx2].T
    gj = gr1 / (np.max(np.abs(gr1), axis=1, keepdims=True) + 0.2) * f64(cb)
    ujq = mxq(uj, 0, "e4m3")
    gjq = mxq(gj, 0, "e5m2")
    w = ujq.T @ gjq
    wq = mxq(w, 0, "e5m2")
    v2 = dru.T @ wq
    wp = np.zeros((R, Q))
    wp[:, idx3] = v2
    y = 0.05 * wp + f64(old)
    return y

@@ -1,0 +1,223 @@
+from contextlib import ExitStack
+
+import concourse.mybir as mybir
+from concourse.masks import make_identity
+
+K, J, N, R, T, V, Q = 512, 512, 256, 256, 1024, 1024, 1024
+FLOPS = 2 * K * J * N + 2 * K * R * N
+
+F32 = mybir.dt.float32
+BF16 = mybir.dt.bfloat16
+I32 = mybir.dt.int32
+U32 = mybir.dt.uint32
+U16 = mybir.dt.uint16
+U8 = mybir.dt.uint8
+E4M3 = mybir.dt.float8_e4m3fn_x4
+E5M2 = mybir.dt.float8_e5m2_x4
+ALU = mybir.AluOpType
+ACT = mybir.ActivationFunctionType
+AXIS_X = mybir.AxisListType.X
+
+P = 128
+PACK = 4
+GROUP = 8
+OUT_CHUNK = 512
+
+
+def tile_list_directions_centred_sized_placed_kernel(
+    tc, xf, ra, gt, cb, fkr, dr_words, dr_scales, old, offs, offs2, offs3, out
+):
+    nc = tc.nc
+    with ExitStack() as ctx:
+        sb = ctx.enter_context(tc.tile_pool(name="sb", bufs=1))
+        shared = ctx.enter_context(tc.tile_pool(name="shared", bufs=1))
+        ps = ctx.enter_context(tc.psum_pool(name="ps", bufs=1))
+
+        def tiles(name, count, shape, dtype):
+            return [sb.tile(shape, dtype, name="%s%d" % (name, i), tag="%s%d" % (name, i), align_bytes=64) for i in range(count)]
+
+        x_list = sb.tile([P, J // 16], U16, name="x_list")
+        g_list = sb.tile([P, J // 16], U16, name="g_list")
+        q_list = sb.tile([P, N // 16], U16, name="q_list")
+        row_bytes, picked_bytes = 4 * T, 4 * J
+        g_rows = [shared.tile([P, V], F32, name="g_rows%d" % h, offset=(2 + h) * row_bytes) for h in range(2)]
+        x_rows = [
+            shared.tile([P, T], F32, name="x_rows%d" % c, offset=place * row_bytes) for c, place in enumerate((0, 1, 4, 5))
+        ]
+        old_rows = tiles("old_rows", 2, [P, Q], F32)
+        placed = tiles("placed", 2, [P, Q], F32)
+        fkr_col = sb.tile([P, PACK], F32, name="fkr_col", tag="sums0", align_bytes=64)
+        ra_col = sb.tile([P, PACK], F32, name="ra_col")
+        cb_col = sb.tile([P, PACK], F32, name="cb_col")
+        ident = sb.tile([P, P], F32, name="ident")
+        dr_codes = sb.tile([P, R], U32, name="dr_codes", align_bytes=64)
+        dr_plane = sb.tile([P, R], U8, name="dr_plane", align_bytes=64)
+
+        ident_bf16 = sb.tile([P, P], BF16, name="ident_bf16", tag="x_picked0", align_bytes=64)
+        make_identity(nc, ident_bf16[:])
+        nc.scalar.activation(ident[:], ident_bf16[:], ACT.Copy)
+        nc.vector.memset(dr_plane[:].bitcast(U32), 0)
+        for r in range(2):
+            nc.vector.memset(placed[r][:], 0.0)
+
+        xf_dealt = xf.rearrange("(p c) t -> c p t", c=PACK)
+        nc.scalar.dma_start(fkr_col[:], fkr.rearrange("o (p c) -> p (o c)", c=PACK))
+        nc.scalar.dma_start(ra_col[:], ra.rearrange("o (p i) -> p (o i)", i=PACK))
+        nc.sync.dma_start(x_list[:], offs)
+        nc.sync.dma_start(x_rows[0][:], xf_dealt[0])
+        nc.sync.dma_start(x_rows[1][:], xf_dealt[1])
+        nc.sync.dma_start(g_list[:], offs2)
+        nc.sync.dma_start(g_rows[0][:], gt[0:P, :])
+        nc.sync.dma_start(g_rows[1][:], gt[P : 2 * P, :])
+        nc.sync.dma_start(cb_col[:], cb.rearrange("(p i) o -> p (i o)", i=PACK))
+        nc.sync.dma_start(x_rows[2][:], xf_dealt[2])
+        nc.sync.dma_start(x_rows[3][:], xf_dealt[3])
+        nc.sync.dma_start(q_list[:], offs3)
+        nc.sync.dma_start(dr_codes[:].bitcast(I32), dr_words[0].rearrange("p n t -> p (n t)").bitcast(I32))
+        for quad in range(4):
+            nc.sync.dma_start(
+                dr_plane[32 * quad : 32 * quad + 4, :].bitcast(I32),
+                dr_scales[0, 4 * quad : 4 * quad + 4, :].bitcast(I32),
+            )
+        for r in range(2):
+            nc.sync.dma_start(old_rows[r][:], old[r * P : (r + 1) * P, :])
+
+        fkr_spread = ps.tile([P, PACK, P], F32, name="fkr_spread", tag="v0")
+        for c in range(PACK):
+            nc.tensor.transpose(fkr_spread[:, c, :], fkr_col[:, c : c + 1].to_broadcast([P, P]), ident[:])
+        weight = tiles("weight", PACK, [P, P, PACK], F32)
+
+        def make_weight(c):
+            nc.vector.tensor_tensor(
+                weight[c][:],
+                fkr_spread[:, c, :].unsqueeze(2).to_broadcast([P, P, PACK]),
+                ra_col[:].unsqueeze(1).to_broadcast([P, P, PACK]),
+                ALU.mult,
+            )
+
+        x_picked = [sb.tile([P, J], F32, name="x_picked0", tag="x_picked0", align_bytes=64)] + [
+            shared.tile([P, J], F32, name="x_picked%d" % c, offset=place * picked_bytes) for c, place in ((1, 0), (2, 3), (3, 4))
+        ]
+        g_picked = [shared.tile([P, J], F32, name="g_picked%d" % h, offset=(1 + h) * picked_bytes) for h in range(2)]
+        neg_mean = tiles("neg_mean", PACK, [P, J // GROUP, 2], F32)
+        u_in = tiles("u_in", PACK, [P, P, PACK], BF16)
+        u_codes = tiles("u_codes", PACK, [P, P], U32)
+        u_plane = tiles("u_plane", PACK, [P, P], U8)
+        g_abs = tiles("g_abs", 2, [P, PACK, P], F32)
+        g_max = tiles("g_max", 2, [P, PACK], F32)
+        g_in = tiles("g_in", 2, [P, P, PACK], BF16)
+        g_codes = tiles("g_codes", 2, [P, P], U32)
+        g_plane = tiles("g_plane", 2, [P, P], U8)
+        g_turned = [ps.tile([P, PACK, P], F32, name="g_turned%d" % h) for h in range(2)]
+        w_bank = [ps.tile([P, PACK, P], F32, name="w_bank%d" % h) for h in range(2)]
+        x_turned = {}
+
+        def pick_g(h):
+            nc.scalar.activation(g_picked[h][:], g_rows[h][:].indirect(g_list[:]), ACT.Copy)
+            for i in range(PACK):
+                nc.tensor.transpose(g_turned[h][:, i, :], g_picked[h][:, i:J:PACK], ident[:])
+
+        def size_g(h):
+            nc.scalar.activation(g_abs[h][:], g_turned[h][:], ACT.Abs)
+            nc.vector.tensor_reduce(g_max[h][:], g_abs[h][:], AXIS_X, ALU.max)
+
+        def pick_x(c):
+            nc.scalar.activation(x_picked[c][:], x_rows[c][:].indirect(x_list[:]), ACT.Copy)
+            sums = sb.tile([P, J // GROUP], F32, name="sums%d" % c, tag="sums%d" % c, align_bytes=64)
+            nc.vector.tensor_reduce(
+                sums[:], x_picked[c][:].rearrange("p (b i) -> p b i", i=GROUP), AXIS_X, ALU.add
+            )
+            nc.gpsimd.tensor_scalar(
+                neg_mean[c][:], sums[:].unsqueeze(2).to_broadcast([P, J // GROUP, 2]), -1.0 / GROUP, 0.0, ALU.mult, ALU.add
+            )
+            x_turned[c] = ps.tile([P, PACK, P], F32, name="x_turned%d" % c, tag="x_turned%d" % (c % 2))
+            for i in range(PACK):
+                nc.tensor.matmul(
+                    x_turned[c][:, i, :], x_picked[c][:, i:J:PACK], ident[:],
+                    start=(i == 0), stop=False, is_transpose=True,
+                )
+            for i in range(PACK):
+                nc.tensor.matmul(
+                    x_turned[c][:, i, :], neg_mean[c][:].rearrange("p b e -> p (b e)"), ident[:],
+                    start=False, stop=(i == PACK - 1), is_transpose=True,
+                )
+
+        def weigh_x(c):
+            nc.vector.tensor_tensor(u_in[c][:], x_turned[c][:].rearrange("p i m -> p m i"), weight[c][:], ALU.mult)
+
+        def quantise(codes, plane, values, fmt):
+            nc.vector.quantize_mx(out=codes[:].bitcast(fmt), scales=plane[:], in_=values[:].rearrange("p m i -> p (m i)"))
+
+        def moment(c):
+            for h in range(2):
+                nc.tensor.matmul_mx(
+                    out=w_bank[h][:, c, :], lhsT=u_codes[c][:].bitcast(E4M3), lhsT_scale=u_plane[c][:],
+                    rhs=g_codes[h][:].bitcast(E5M2), rhs_scale=g_plane[h][:], start=True, stop=True,
+                )
+
+        max0_plus = sb.tile([P, PACK], F32, name="max0_plus")
+        denom = sb.tile([P, PACK], F32, name="denom")
+        inv = sb.tile([P, PACK], F32, name="inv")
+        g_factor = sb.tile([P, PACK], F32, name="g_factor")
+
+        make_weight(0)
+        make_weight(1)
+        pick_x(0)
+        make_weight(2)
+        pick_x(1)
+        weigh_x(0)
+        pick_g(0)
+        make_weight(3)
+        pick_g(1)
+        weigh_x(1)
+        quantise(u_codes[0], u_plane[0], u_in[0], E4M3)
+        size_g(0)
+        quantise(u_codes[1], u_plane[1], u_in[1], E4M3)
+        size_g(1)
+        nc.vector.tensor_scalar(max0_plus[:], g_max[0][:], 0.2, None, ALU.add)
+        nc.vector.scalar_tensor_tensor(denom[:], g_max[1][:], 0.2, max0_plus[:], ALU.add, ALU.max)
+        nc.vector.reciprocal(inv[:], denom[:])
+        pick_x(2)
+        nc.vector.tensor_tensor(g_factor[:], inv[:], cb_col[:], ALU.mult)
+        for h in range(2):
+            nc.vector.tensor_tensor(
+                g_in[h][:], g_turned[h][:].rearrange("p i n -> p n i"),
+                g_factor[:].unsqueeze(1).to_broadcast([P, P, PACK]), ALU.mult,
+            )
+        pick_x(3)
+        weigh_x(2)
+        for h in range(2):
+            quantise(g_codes[h], g_plane[h], g_in[h], E5M2)
+        quantise(u_codes[2], u_plane[2], u_in[2], E4M3)
+        weigh_x(3)
+        quantise(u_codes[3], u_plane[3], u_in[3], E4M3)
+        for c in range(PACK):
+            moment(c)
+
+        w_in = tiles("w_in", 2, [P, P, PACK], BF16)
+        w_codes = tiles("w_codes", 2, [P, P], U32)
+        w_plane = tiles("w_plane", 2, [P, P], U8)
+        nc.vector.tensor_copy(w_in[0][:], w_bank[0][:].rearrange("p c n -> p n c"))
+        nc.scalar.copy(w_in[1][:], w_bank[1][:].rearrange("p c n -> p n c"))
+        for h in (1, 0):
+            quantise(w_codes[h], w_plane[h], w_in[h], E5M2)
+        v_bank = [ps.tile([P, N], F32, name="v_bank%d" % r, tag="v%d" % r) for r in range(2)]
+        for h in (1, 0):
+            for r in range(2):
+                nc.tensor.matmul_mx(
+                    out=v_bank[r][:, h * P : (h + 1) * P],
+                    lhsT=dr_codes[:, r * P : (r + 1) * P].bitcast(E4M3), lhsT_scale=dr_plane[:, r * P : (r + 1) * P],
+                    rhs=w_codes[h][:].bitcast(E5M2), rhs_scale=w_plane[h][:], start=True, stop=True,
+                )
+        v_rows = tiles("v_rows", 2, [P, N], F32)
+        nc.vector.tensor_copy(v_rows[0][:], v_bank[0][:])
+        nc.scalar.copy(v_rows[1][:], v_bank[1][:])
+        nc.vector.tensor_copy(placed[0][:].indirect(q_list[:]), v_rows[0][:])
+        nc.scalar.activation(placed[1][:].indirect(q_list[:]), v_rows[1][:], ACT.Copy)
+        for r in range(2):
+            edges = (0, 512, 1024) if r == 0 else (0, 512, 768, 1024)
+            for q0, q1 in zip(edges, edges[1:]):
+                cols = slice(q0, q1)
+                result = sb.tile([P, q1 - q0], F32, name="result%d_%d" % (r, q0))
+                nc.vector.scalar_tensor_tensor(result[:], placed[r][:, cols], 0.05, old_rows[r][:, cols], ALU.mult, ALU.add)
+                nc.sync.dma_start(out[r * P : (r + 1) * P, cols], result[:])

@@ -1,7 +1,6 @@
 from contextlib import ExitStack
 
 import concourse.mybir as mybir
-from concourse.masks import make_identity
 
 K, J, N, R, T, V, Q = 512, 512, 256, 256, 1024, 1024, 1024
 FLOPS = 2 * K * J * N + 2 * K * R * N
@@ -30,7 +29,6 @@ def tile_list_directions_centred_sized_placed_kernel(
     nc = tc.nc
     with ExitStack() as ctx:
         sb = ctx.enter_context(tc.tile_pool(name="sb", bufs=1))
-        shared = ctx.enter_context(tc.tile_pool(name="shared", bufs=1))
         ps = ctx.enter_context(tc.psum_pool(name="ps", bufs=1))
 
         def tiles(name, count, shape, dtype):
@@ -39,39 +37,43 @@ def tile_list_directions_centred_sized_placed_kernel(
         x_list = sb.tile([P, J // 16], U16, name="x_list")
         g_list = sb.tile([P, J // 16], U16, name="g_list")
         q_list = sb.tile([P, N // 16], U16, name="q_list")
-        row_bytes, picked_bytes = 4 * T, 4 * J
-        g_rows = [shared.tile([P, V], F32, name="g_rows%d" % h, offset=(2 + h) * row_bytes) for h in range(2)]
-        x_rows = [
-            shared.tile([P, T], F32, name="x_rows%d" % c, offset=place * row_bytes) for c, place in enumerate((0, 1, 4, 5))
-        ]
+        g_rows = tiles("g_rows", 2, [P, V], F32)
+        x_rows = tiles("x_rows", PACK, [P, T], F32)
         old_rows = tiles("old_rows", 2, [P, Q], F32)
-        placed = tiles("placed", 2, [P, Q], F32)
-        fkr_col = sb.tile([P, PACK], F32, name="fkr_col", tag="sums0", align_bytes=64)
+        fkr_col = sb.tile([P, PACK], F32, name="fkr_col")
         ra_col = sb.tile([P, PACK], F32, name="ra_col")
         cb_col = sb.tile([P, PACK], F32, name="cb_col")
         ident = sb.tile([P, P], F32, name="ident")
         dr_codes = sb.tile([P, R], U32, name="dr_codes", align_bytes=64)
         dr_plane = sb.tile([P, R], U8, name="dr_plane", align_bytes=64)
 
-        ident_bf16 = sb.tile([P, P], BF16, name="ident_bf16", tag="x_picked0", align_bytes=64)
-        make_identity(nc, ident_bf16[:])
-        nc.scalar.activation(ident[:], ident_bf16[:], ACT.Copy)
-        nc.vector.memset(dr_plane[:].bitcast(U32), 0)
-        for r in range(2):
-            nc.vector.memset(placed[r][:], 0.0)
-
-        xf_dealt = xf.rearrange("(p c) t -> c p t", c=PACK)
+        ones = sb.tile([P, P], F32, name="ones")
+        column = sb.tile([P, P], F32, name="column", tag="placed0", align_bytes=64)
+        row_in_quad = sb.tile([P, 32], F32, name="row_in_quad", tag="placed1", align_bytes=64)
+        quad_start = sb.tile([P, 1], F32, name="quad_start")
+        fifth = sb.tile([P, 1], F32, name="fifth")
         nc.scalar.dma_start(fkr_col[:], fkr.rearrange("o (p c) -> p (o c)", c=PACK))
         nc.scalar.dma_start(ra_col[:], ra.rearrange("o (p i) -> p (o i)", i=PACK))
-        nc.sync.dma_start(x_list[:], offs)
-        nc.sync.dma_start(x_rows[0][:], xf_dealt[0])
-        nc.sync.dma_start(x_rows[1][:], xf_dealt[1])
+        nc.scalar.dma_start(cb_col[:], cb.rearrange("(p i) o -> p (i o)", i=PACK))
+        nc.vector.memset(ones[:], 1.0)
+        nc.scalar.activation(fifth[:], ones[:, 0:1], ACT.Copy, scale=0.2)
+        nc.vector.tensor_tensor_scan(column[:], ones[:], ones[:], 0.0, ALU.mult, ALU.add)
+        for quad in range(4):
+            nc.vector.memset(quad_start[32 * quad : 32 * quad + 32, :], 32.0 * quad)
+        nc.vector.transpose(row_in_quad[:], column[:, 0:32])
+        nc.vector.memset(dr_plane[:].bitcast(U32), 0)
+        nc.vector.tensor_scalar(ident[:], column[:], row_in_quad[:, 0:1], quad_start[:], ALU.subtract, ALU.is_equal)
+        placed = tiles("placed", 2, [P, Q], F32)
+        for r in range(2):
+            nc.gpsimd.memset(placed[r][:], 0.0)
+
+        xf_dealt = xf.rearrange("(p c) t -> c p t", c=PACK)
         nc.sync.dma_start(g_list[:], offs2)
-        nc.sync.dma_start(g_rows[0][:], gt[0:P, :])
-        nc.sync.dma_start(g_rows[1][:], gt[P : 2 * P, :])
-        nc.sync.dma_start(cb_col[:], cb.rearrange("(p i) o -> p (i o)", i=PACK))
-        nc.sync.dma_start(x_rows[2][:], xf_dealt[2])
-        nc.sync.dma_start(x_rows[3][:], xf_dealt[3])
+        nc.sync.dma_start(x_list[:], offs)
+        for h in range(2):
+            nc.sync.dma_start(g_rows[h][:], gt[h * P : (h + 1) * P, :])
+        for c in range(PACK):
+            nc.sync.dma_start(x_rows[c][:], xf_dealt[c])
         nc.sync.dma_start(q_list[:], offs3)
         nc.sync.dma_start(dr_codes[:].bitcast(I32), dr_words[0].rearrange("p n t -> p (n t)").bitcast(I32))
         for quad in range(4):
@@ -82,7 +84,7 @@ def tile_list_directions_centred_sized_placed_kernel(
         for r in range(2):
             nc.sync.dma_start(old_rows[r][:], old[r * P : (r + 1) * P, :])
 
-        fkr_spread = ps.tile([P, PACK, P], F32, name="fkr_spread", tag="v0")
+        fkr_spread = ps.tile([P, PACK, P], F32, name="fkr_spread", tag="w_bank0")
         for c in range(PACK):
             nc.tensor.transpose(fkr_spread[:, c, :], fkr_col[:, c : c + 1].to_broadcast([P, P]), ident[:])
         weight = tiles("weight", PACK, [P, P, PACK], F32)
@@ -95,42 +97,45 @@ def tile_list_directions_centred_sized_placed_kernel(
                 ALU.mult,
             )
 
-        x_picked = [sb.tile([P, J], F32, name="x_picked0", tag="x_picked0", align_bytes=64)] + [
-            shared.tile([P, J], F32, name="x_picked%d" % c, offset=place * picked_bytes) for c, place in ((1, 0), (2, 3), (3, 4))
-        ]
-        g_picked = [shared.tile([P, J], F32, name="g_picked%d" % h, offset=(1 + h) * picked_bytes) for h in range(2)]
+        x_picked = tiles("x_picked", PACK, [P, J], F32)
+        g_picked = tiles("g_picked", 2, [P, J], F32)
         neg_mean = tiles("neg_mean", PACK, [P, J // GROUP, 2], F32)
         u_in = tiles("u_in", PACK, [P, P, PACK], BF16)
         u_codes = tiles("u_codes", PACK, [P, P], U32)
         u_plane = tiles("u_plane", PACK, [P, P], U8)
-        g_abs = tiles("g_abs", 2, [P, PACK, P], F32)
         g_max = tiles("g_max", 2, [P, PACK], F32)
         g_in = tiles("g_in", 2, [P, P, PACK], BF16)
         g_codes = tiles("g_codes", 2, [P, P], U32)
         g_plane = tiles("g_plane", 2, [P, P], U8)
-        g_turned = [ps.tile([P, PACK, P], F32, name="g_turned%d" % h) for h in range(2)]
-        w_bank = [ps.tile([P, PACK, P], F32, name="w_bank%d" % h) for h in range(2)]
+        g_turned = {}
         x_turned = {}
 
         def pick_g(h):
             nc.scalar.activation(g_picked[h][:], g_rows[h][:].indirect(g_list[:]), ACT.Copy)
+            g_turned[h] = ps.tile([P, PACK, P], F32, name="g_turned%d" % h, tag="g_turned%d" % h)
             for i in range(PACK):
                 nc.tensor.transpose(g_turned[h][:, i, :], g_picked[h][:, i:J:PACK], ident[:])
 
         def size_g(h):
-            nc.scalar.activation(g_abs[h][:], g_turned[h][:], ACT.Abs)
-            nc.vector.tensor_reduce(g_max[h][:], g_abs[h][:], AXIS_X, ALU.max)
+            g_abs = sb.tile([P, PACK, P], F32, name="g_abs%d" % h, tag=("g_rows1", "x_rows1")[h], align_bytes=64)
+            nc.scalar.activation(g_abs[:], g_turned[h][:], ACT.Abs)
+            nc.vector.tensor_reduce(g_max[h][:], g_abs[:], AXIS_X, ALU.max)
 
         def pick_x(c):
-            nc.scalar.activation(x_picked[c][:], x_rows[c][:].indirect(x_list[:]), ACT.Copy)
+            if c == 0:
+                nc.vector.tensor_copy(x_picked[c][:], x_rows[c][:].indirect(x_list[:]))
+            else:
+                nc.scalar.activation(x_picked[c][:], x_rows[c][:].indirect(x_list[:]), ACT.Copy)
             sums = sb.tile([P, J // GROUP], F32, name="sums%d" % c, tag="sums%d" % c, align_bytes=64)
             nc.vector.tensor_reduce(
                 sums[:], x_picked[c][:].rearrange("p (b i) -> p b i", i=GROUP), AXIS_X, ALU.add
             )
-            nc.gpsimd.tensor_scalar(
-                neg_mean[c][:], sums[:].unsqueeze(2).to_broadcast([P, J // GROUP, 2]), -1.0 / GROUP, 0.0, ALU.mult, ALU.add
-            )
-            x_turned[c] = ps.tile([P, PACK, P], F32, name="x_turned%d" % c, tag="x_turned%d" % (c % 2))
+            twice = sums[:].unsqueeze(2).to_broadcast([P, J // GROUP, 2])
+            if c < 2:
+                nc.vector.tensor_scalar(neg_mean[c][:], twice, -1.0 / GROUP, None, ALU.mult)
+            else:
+                nc.scalar.activation(neg_mean[c][:], twice, ACT.Copy, scale=-1.0 / GROUP)
+            x_turned[c] = ps.tile([P, PACK, P], F32, name="x_turned%d" % c, tag="x_turned%d" % c)
             for i in range(PACK):
                 nc.tensor.matmul(
                     x_turned[c][:, i, :], x_picked[c][:, i:J:PACK], ident[:],
@@ -160,37 +165,37 @@ def tile_list_directions_centred_sized_placed_kernel(
         inv = sb.tile([P, PACK], F32, name="inv")
         g_factor = sb.tile([P, PACK], F32, name="g_factor")
 
-        make_weight(0)
-        make_weight(1)
-        pick_x(0)
-        make_weight(2)
-        pick_x(1)
-        weigh_x(0)
+        for c in range(PACK):
+            make_weight(c)
         pick_g(0)
-        make_weight(3)
         pick_g(1)
-        weigh_x(1)
-        quantise(u_codes[0], u_plane[0], u_in[0], E4M3)
+        pick_x(0)
         size_g(0)
-        quantise(u_codes[1], u_plane[1], u_in[1], E4M3)
+        pick_x(1)
         size_g(1)
-        nc.vector.tensor_scalar(max0_plus[:], g_max[0][:], 0.2, None, ALU.add)
-        nc.vector.scalar_tensor_tensor(denom[:], g_max[1][:], 0.2, max0_plus[:], ALU.add, ALU.max)
+        nc.vector.tensor_scalar(max0_plus[:], g_max[0][:], fifth[:], None, ALU.add)
+        nc.vector.scalar_tensor_tensor(denom[:], g_max[1][:], fifth[:], max0_plus[:], ALU.add, ALU.max)
         nc.vector.reciprocal(inv[:], denom[:])
-        pick_x(2)
         nc.vector.tensor_tensor(g_factor[:], inv[:], cb_col[:], ALU.mult)
-        for h in range(2):
-            nc.vector.tensor_tensor(
-                g_in[h][:], g_turned[h][:].rearrange("p i n -> p n i"),
-                g_factor[:].unsqueeze(1).to_broadcast([P, P, PACK]), ALU.mult,
-            )
+        pick_x(2)
+        weigh_x(0)
         pick_x(3)
-        weigh_x(2)
+        weigh_x(1)
+        nc.vector.tensor_tensor(
+            g_in[0][:], g_turned[0][:].rearrange("p i n -> p n i"),
+            g_factor[:].unsqueeze(1).to_broadcast([P, P, PACK]), ALU.mult,
+        )
+        for i in range(PACK):
+            nc.scalar.activation(g_in[1][:, :, i], g_turned[1][:, i, :], ACT.Copy, scale=g_factor[:, i : i + 1])
+        for c in range(2):
+            quantise(u_codes[c], u_plane[c], u_in[c], E4M3)
         for h in range(2):
             quantise(g_codes[h], g_plane[h], g_in[h], E5M2)
-        quantise(u_codes[2], u_plane[2], u_in[2], E4M3)
-        weigh_x(3)
-        quantise(u_codes[3], u_plane[3], u_in[3], E4M3)
+        for c in range(2, PACK):
+            weigh_x(c)
+        for c in range(2, PACK):
+            quantise(u_codes[c], u_plane[c], u_in[c], E4M3)
+        w_bank = [ps.tile([P, PACK, P], F32, name="w_bank%d" % h, tag="w_bank%d" % h) for h in range(2)]
         for c in range(PACK):
             moment(c)
 
@@ -201,9 +206,9 @@ def tile_list_directions_centred_sized_placed_kernel(
         nc.scalar.copy(w_in[1][:], w_bank[1][:].rearrange("p c n -> p n c"))
         for h in (1, 0):
             quantise(w_codes[h], w_plane[h], w_in[h], E5M2)
-        v_bank = [ps.tile([P, N], F32, name="v_bank%d" % r, tag="v%d" % r) for r in range(2)]
-        for h in (1, 0):
-            for r in range(2):
+        v_bank = [ps.tile([P, N], F32, name="v_bank%d" % r, tag="g_turned%d" % r) for r in range(2)]
+        for r in range(2):
+            for h in (1, 0):
                 nc.tensor.matmul_mx(
                     out=v_bank[r][:, h * P : (h + 1) * P],
                     lhsT=dr_codes[:, r * P : (r + 1) * P].bitcast(E4M3), lhsT_scale=dr_plane[:, r * P : (r + 1) * P],

@@ -29,6 +29,7 @@ def tile_list_directions_centred_sized_placed_kernel(
     nc = tc.nc
     with ExitStack() as ctx:
         sb = ctx.enter_context(tc.tile_pool(name="sb", bufs=1))
+        reused = ctx.enter_context(tc.tile_pool(name="reused", bufs=1))
         ps = ctx.enter_context(tc.psum_pool(name="ps", bufs=1))
 
         def tiles(name, count, shape, dtype):
@@ -39,6 +40,7 @@ def tile_list_directions_centred_sized_placed_kernel(
         q_list = sb.tile([P, N // 16], U16, name="q_list")
         g_rows = tiles("g_rows", 2, [P, V], F32)
         x_rows = tiles("x_rows", PACK, [P, T], F32)
+        x_rows[1] = reused.tile([P, T], F32, name="x_rows1_reused", offset=0)
         old_rows = tiles("old_rows", 2, [P, Q], F32)
         fkr_col = sb.tile([P, PACK], F32, name="fkr_col")
         ra_col = sb.tile([P, PACK], F32, name="ra_col")
@@ -98,6 +100,7 @@ def tile_list_directions_centred_sized_placed_kernel(
             )
 
         x_picked = tiles("x_picked", PACK, [P, J], F32)
+        x_picked[2] = reused.tile([P, J], F32, name="x_picked2_reused", offset=4 * J)
         g_picked = tiles("g_picked", 2, [P, J], F32)
         neg_mean = tiles("neg_mean", PACK, [P, J // GROUP, 2], F32)
         u_in = tiles("u_in", PACK, [P, P, PACK], BF16)
@@ -117,7 +120,10 @@ def tile_list_directions_centred_sized_placed_kernel(
                 nc.tensor.transpose(g_turned[h][:, i, :], g_picked[h][:, i:J:PACK], ident[:])
 
         def size_g(h):
-            g_abs = sb.tile([P, PACK, P], F32, name="g_abs%d" % h, tag=("g_rows1", "x_rows1")[h], align_bytes=64)
+            if h == 0:
+                g_abs = sb.tile([P, PACK, P], F32, name="g_abs0", tag="g_rows1", align_bytes=64)
+            else:
+                g_abs = reused.tile([P, PACK, P], F32, name="g_abs1", offset=0)
             nc.scalar.activation(g_abs[:], g_turned[h][:], ACT.Abs)
             nc.vector.tensor_reduce(g_max[h][:], g_abs[:], AXIS_X, ALU.max)
 
@@ -134,7 +140,7 @@ def tile_list_directions_centred_sized_placed_kernel(
             if c < 2:
                 nc.vector.tensor_scalar(neg_mean[c][:], twice, -1.0 / GROUP, None, ALU.mult)
             else:
-                nc.scalar.activation(neg_mean[c][:], twice, ACT.Copy, scale=-1.0 / GROUP)
+                nc.gpsimd.tensor_scalar(neg_mean[c][:], twice, -1.0 / GROUP, 0.0, ALU.mult, ALU.add)
             x_turned[c] = ps.tile([P, PACK, P], F32, name="x_turned%d" % c, tag="x_turned%d" % c)
             for i in range(PACK):
                 nc.tensor.matmul(
@@ -215,12 +221,12 @@ def tile_list_directions_centred_sized_placed_kernel(
                     rhs=w_codes[h][:].bitcast(E5M2), rhs_scale=w_plane[h][:], start=True, stop=True,
                 )
         v_rows = tiles("v_rows", 2, [P, N], F32)
-        nc.vector.tensor_copy(v_rows[0][:], v_bank[0][:])
-        nc.scalar.copy(v_rows[1][:], v_bank[1][:])
+        for r in range(2):
+            nc.scalar.copy(v_rows[r][:], v_bank[r][:])
         nc.vector.tensor_copy(placed[0][:].indirect(q_list[:]), v_rows[0][:])
         nc.scalar.activation(placed[1][:].indirect(q_list[:]), v_rows[1][:], ACT.Copy)
         for r in range(2):
-            edges = (0, 512, 1024) if r == 0 else (0, 512, 768, 1024)
+            edges = (0, 256, 512, 1024) if r == 0 else (0, 512, 768, 1024)
             for q0, q1 in zip(edges, edges[1:]):
                 cols = slice(q0, q1)
                 result = sb.tile([P, q1 - q0], F32, name="result%d_%d" % (r, q0))

@@ -44,7 +44,7 @@ def tile_list_directions_centred_sized_placed_kernel(
         old_rows = tiles("old_rows", 2, [P, Q], F32)
         fkr_col = sb.tile([P, PACK], F32, name="fkr_col")
         ra_col = sb.tile([P, PACK], F32, name="ra_col")
-        cb_col = sb.tile([P, PACK], F32, name="cb_col")
+        cb_col = sb.tile([P, PACK], F32, name="cb_col", tag="u_in0", align_bytes=64)
         ident = sb.tile([P, P], F32, name="ident")
         dr_codes = sb.tile([P, R], U32, name="dr_codes", align_bytes=64)
         dr_plane = sb.tile([P, R], U8, name="dr_plane", align_bytes=64)
@@ -103,7 +103,7 @@ def tile_list_directions_centred_sized_placed_kernel(
         x_picked[2] = reused.tile([P, J], F32, name="x_picked2_reused", offset=4 * J)
         g_picked = tiles("g_picked", 2, [P, J], F32)
         neg_mean = tiles("neg_mean", PACK, [P, J // GROUP, 2], F32)
-        u_in = tiles("u_in", PACK, [P, P, PACK], BF16)
+        u_in = {}
         u_codes = tiles("u_codes", PACK, [P, P], U32)
         u_plane = tiles("u_plane", PACK, [P, P], U8)
         g_max = tiles("g_max", 2, [P, PACK], F32)
@@ -154,6 +154,7 @@ def tile_list_directions_centred_sized_placed_kernel(
                 )
 
         def weigh_x(c):
+            u_in[c] = sb.tile([P, P, PACK], BF16, name="u_in%d" % c, tag="weight0" if c == 1 else "u_in%d" % c, align_bytes=64)
             nc.vector.tensor_tensor(u_in[c][:], x_turned[c][:].rearrange("p i m -> p m i"), weight[c][:], ALU.mult)
 
         def quantise(codes, plane, values, fmt):
@@ -167,7 +168,7 @@ def tile_list_directions_centred_sized_placed_kernel(
                 )
 
         max0_plus = sb.tile([P, PACK], F32, name="max0_plus")
-        denom = sb.tile([P, PACK], F32, name="denom")
+        denom = sb.tile([P, PACK], F32, name="denom", tag="sums2", align_bytes=64)
         inv = sb.tile([P, PACK], F32, name="inv")
         g_factor = sb.tile([P, PACK], F32, name="g_factor")
 
@@ -212,21 +213,20 @@ def tile_list_directions_centred_sized_placed_kernel(
         nc.scalar.copy(w_in[1][:], w_bank[1][:].rearrange("p c n -> p n c"))
         for h in (1, 0):
             quantise(w_codes[h], w_plane[h], w_in[h], E5M2)
-        v_bank = [ps.tile([P, N], F32, name="v_bank%d" % r, tag="g_turned%d" % r) for r in range(2)]
+        v_rows = tiles("v_rows", 2, [P, N], F32)
         for r in range(2):
             for h in (1, 0):
+                v_bank = ps.tile([P, P], F32, name="v_bank%d_%d" % (r, h), tag="x_turned%d" % (2 * r + h))
                 nc.tensor.matmul_mx(
-                    out=v_bank[r][:, h * P : (h + 1) * P],
+                    out=v_bank[:],
                     lhsT=dr_codes[:, r * P : (r + 1) * P].bitcast(E4M3), lhsT_scale=dr_plane[:, r * P : (r + 1) * P],
                     rhs=w_codes[h][:].bitcast(E5M2), rhs_scale=w_plane[h][:], start=True, stop=True,
                 )
-        v_rows = tiles("v_rows", 2, [P, N], F32)
-        for r in range(2):
-            nc.scalar.copy(v_rows[r][:], v_bank[r][:])
+                nc.scalar.copy(v_rows[r][:, h * P : (h + 1) * P], v_bank[:])
         nc.vector.tensor_copy(placed[0][:].indirect(q_list[:]), v_rows[0][:])
         nc.scalar.activation(placed[1][:].indirect(q_list[:]), v_rows[1][:], ACT.Copy)
         for r in range(2):
-            edges = (0, 256, 512, 1024) if r == 0 else (0, 512, 768, 1024)
+            edges = (0, 512, 1024) if r == 0 else (0, 512, 896, 1024)
             for q0, q1 in zip(edges, edges[1:]):
                 cols = slice(q0, q1)
                 result = sb.tile([P, q1 - q0], F32, name="result%d_%d" % (r, q0))

from contextlib import ExitStack

import concourse.mybir as mybir

K, J, N, R, T, V, Q = 512, 512, 256, 256, 1024, 1024, 1024
FLOPS = 2 * K * J * N + 2 * K * R * N

F32 = mybir.dt.float32
BF16 = mybir.dt.bfloat16
I32 = mybir.dt.int32
U32 = mybir.dt.uint32
U16 = mybir.dt.uint16
U8 = mybir.dt.uint8
E4M3 = mybir.dt.float8_e4m3fn_x4
E5M2 = mybir.dt.float8_e5m2_x4
ALU = mybir.AluOpType
ACT = mybir.ActivationFunctionType
AXIS_X = mybir.AxisListType.X

P = 128
PACK = 4
GROUP = 8
OUT_CHUNK = 512


def tile_list_directions_centred_sized_placed_kernel(
    tc, xf, ra, gt, cb, fkr, dr_words, dr_scales, old, offs, offs2, offs3, out
):
    nc = tc.nc
    with ExitStack() as ctx:
        sb = ctx.enter_context(tc.tile_pool(name="sb", bufs=1))
        reused = ctx.enter_context(tc.tile_pool(name="reused", bufs=1))
        ps = ctx.enter_context(tc.psum_pool(name="ps", bufs=1))

        def tiles(name, count, shape, dtype):
            return [sb.tile(shape, dtype, name="%s%d" % (name, i), tag="%s%d" % (name, i), align_bytes=64) for i in range(count)]

        x_list = sb.tile([P, J // 16], U16, name="x_list")
        g_list = sb.tile([P, J // 16], U16, name="g_list")
        q_list = sb.tile([P, N // 16], U16, name="q_list")
        g_rows = tiles("g_rows", 2, [P, V], F32)
        x_rows = tiles("x_rows", PACK, [P, T], F32)
        x_rows[1] = reused.tile([P, T], F32, name="x_rows1_reused", offset=0)
        old_rows = tiles("old_rows", 2, [P, Q], F32)
        fkr_col = sb.tile([P, PACK], F32, name="fkr_col")
        ra_col = sb.tile([P, PACK], F32, name="ra_col")
        cb_col = sb.tile([P, PACK], F32, name="cb_col", tag="u_in0", align_bytes=64)
        ident = sb.tile([P, P], F32, name="ident")
        dr_codes = sb.tile([P, R], U32, name="dr_codes", align_bytes=64)
        dr_plane = sb.tile([P, R], U8, name="dr_plane", align_bytes=64)

        ones = sb.tile([P, P], F32, name="ones")
        column = sb.tile([P, P], F32, name="column", tag="placed0", align_bytes=64)
        row_in_quad = sb.tile([P, 32], F32, name="row_in_quad", tag="placed1", align_bytes=64)
        quad_start = sb.tile([P, 1], F32, name="quad_start")
        fifth = sb.tile([P, 1], F32, name="fifth")
        nc.scalar.dma_start(fkr_col[:], fkr.rearrange("o (p c) -> p (o c)", c=PACK))
        nc.scalar.dma_start(ra_col[:], ra.rearrange("o (p i) -> p (o i)", i=PACK))
        nc.scalar.dma_start(cb_col[:], cb.rearrange("(p i) o -> p (i o)", i=PACK))
        nc.vector.memset(ones[:], 1.0)
        nc.scalar.activation(fifth[:], ones[:, 0:1], ACT.Copy, scale=0.2)
        nc.vector.tensor_tensor_scan(column[:], ones[:], ones[:], 0.0, ALU.mult, ALU.add)
        for quad in range(4):
            nc.vector.memset(quad_start[32 * quad : 32 * quad + 32, :], 32.0 * quad)
        nc.vector.transpose(row_in_quad[:], column[:, 0:32])
        nc.vector.memset(dr_plane[:].bitcast(U32), 0)
        nc.vector.tensor_scalar(ident[:], column[:], row_in_quad[:, 0:1], quad_start[:], ALU.subtract, ALU.is_equal)
        placed = tiles("placed", 2, [P, Q], F32)
        for r in range(2):
            nc.gpsimd.memset(placed[r][:], 0.0)

        xf_dealt = xf.rearrange("(p c) t -> c p t", c=PACK)
        nc.sync.dma_start(g_list[:], offs2)
        nc.sync.dma_start(x_list[:], offs)
        for h in range(2):
            nc.sync.dma_start(g_rows[h][:], gt[h * P : (h + 1) * P, :])
        for c in range(PACK):
            nc.sync.dma_start(x_rows[c][:], xf_dealt[c])
        nc.sync.dma_start(q_list[:], offs3)
        nc.sync.dma_start(dr_codes[:].bitcast(I32), dr_words[0].rearrange("p n t -> p (n t)").bitcast(I32))
        for quad in range(4):
            nc.sync.dma_start(
                dr_plane[32 * quad : 32 * quad + 4, :].bitcast(I32),
                dr_scales[0, 4 * quad : 4 * quad + 4, :].bitcast(I32),
            )
        for r in range(2):
            nc.sync.dma_start(old_rows[r][:], old[r * P : (r + 1) * P, :])

        fkr_spread = ps.tile([P, PACK, P], F32, name="fkr_spread", tag="w_bank0")
        for c in range(PACK):
            nc.tensor.transpose(fkr_spread[:, c, :], fkr_col[:, c : c + 1].to_broadcast([P, P]), ident[:])
        weight = tiles("weight", PACK, [P, P, PACK], F32)

        def make_weight(c):
            nc.vector.tensor_tensor(
                weight[c][:],
                fkr_spread[:, c, :].unsqueeze(2).to_broadcast([P, P, PACK]),
                ra_col[:].unsqueeze(1).to_broadcast([P, P, PACK]),
                ALU.mult,
            )

        x_picked = tiles("x_picked", PACK, [P, J], F32)
        x_picked[2] = reused.tile([P, J], F32, name="x_picked2_reused", offset=4 * J)
        g_picked = tiles("g_picked", 2, [P, J], F32)
        neg_mean = tiles("neg_mean", PACK, [P, J // GROUP, 2], F32)
        u_in = {}
        u_codes = tiles("u_codes", PACK, [P, P], U32)
        u_plane = tiles("u_plane", PACK, [P, P], U8)
        g_max = tiles("g_max", 2, [P, PACK], F32)
        g_in = tiles("g_in", 2, [P, P, PACK], BF16)
        g_codes = tiles("g_codes", 2, [P, P], U32)
        g_plane = tiles("g_plane", 2, [P, P], U8)
        g_turned = {}
        x_turned = {}

        def pick_g(h):
            nc.scalar.activation(g_picked[h][:], g_rows[h][:].indirect(g_list[:]), ACT.Copy)
            g_turned[h] = ps.tile([P, PACK, P], F32, name="g_turned%d" % h, tag="g_turned%d" % h)
            for i in range(PACK):
                nc.tensor.transpose(g_turned[h][:, i, :], g_picked[h][:, i:J:PACK], ident[:])

        def size_g(h):
            if h == 0:
                g_abs = sb.tile([P, PACK, P], F32, name="g_abs0", tag="g_rows1", align_bytes=64)
            else:
                g_abs = reused.tile([P, PACK, P], F32, name="g_abs1", offset=0)
            nc.scalar.activation(g_abs[:], g_turned[h][:], ACT.Abs)
            nc.vector.tensor_reduce(g_max[h][:], g_abs[:], AXIS_X, ALU.max)

        def pick_x(c):
            if c == 0:
                nc.vector.tensor_copy(x_picked[c][:], x_rows[c][:].indirect(x_list[:]))
            else:
                nc.scalar.activation(x_picked[c][:], x_rows[c][:].indirect(x_list[:]), ACT.Copy)
            sums = sb.tile([P, J // GROUP], F32, name="sums%d" % c, tag="sums%d" % c, align_bytes=64)
            nc.vector.tensor_reduce(
                sums[:], x_picked[c][:].rearrange("p (b i) -> p b i", i=GROUP), AXIS_X, ALU.add
            )
            twice = sums[:].unsqueeze(2).to_broadcast([P, J // GROUP, 2])
            if c < 2:
                nc.vector.tensor_scalar(neg_mean[c][:], twice, -1.0 / GROUP, None, ALU.mult)
            else:
                nc.gpsimd.tensor_scalar(neg_mean[c][:], twice, -1.0 / GROUP, 0.0, ALU.mult, ALU.add)
            x_turned[c] = ps.tile([P, PACK, P], F32, name="x_turned%d" % c, tag="x_turned%d" % c)
            for i in range(PACK):
                nc.tensor.matmul(
                    x_turned[c][:, i, :], x_picked[c][:, i:J:PACK], ident[:],
                    start=(i == 0), stop=False, is_transpose=True,
                )
            for i in range(PACK):
                nc.tensor.matmul(
                    x_turned[c][:, i, :], neg_mean[c][:].rearrange("p b e -> p (b e)"), ident[:],
                    start=False, stop=(i == PACK - 1), is_transpose=True,
                )

        def weigh_x(c):
            u_in[c] = sb.tile([P, P, PACK], BF16, name="u_in%d" % c, tag="weight0" if c == 1 else "u_in%d" % c, align_bytes=64)
            nc.vector.tensor_tensor(u_in[c][:], x_turned[c][:].rearrange("p i m -> p m i"), weight[c][:], ALU.mult)

        def quantise(codes, plane, values, fmt):
            nc.vector.quantize_mx(out=codes[:].bitcast(fmt), scales=plane[:], in_=values[:].rearrange("p m i -> p (m i)"))

        def moment(c):
            for h in range(2):
                nc.tensor.matmul_mx(
                    out=w_bank[h][:, c, :], lhsT=u_codes[c][:].bitcast(E4M3), lhsT_scale=u_plane[c][:],
                    rhs=g_codes[h][:].bitcast(E5M2), rhs_scale=g_plane[h][:], start=True, stop=True,
                )

        max0_plus = sb.tile([P, PACK], F32, name="max0_plus")
        denom = sb.tile([P, PACK], F32, name="denom", tag="sums2", align_bytes=64)
        inv = sb.tile([P, PACK], F32, name="inv")
        g_factor = sb.tile([P, PACK], F32, name="g_factor")

        for c in range(PACK):
            make_weight(c)
        pick_g(0)
        pick_g(1)
        pick_x(0)
        size_g(0)
        pick_x(1)
        size_g(1)
        nc.vector.tensor_scalar(max0_plus[:], g_max[0][:], fifth[:], None, ALU.add)
        nc.vector.scalar_tensor_tensor(denom[:], g_max[1][:], fifth[:], max0_plus[:], ALU.add, ALU.max)
        nc.vector.reciprocal(inv[:], denom[:])
        nc.vector.tensor_tensor(g_factor[:], inv[:], cb_col[:], ALU.mult)
        pick_x(2)
        weigh_x(0)
        pick_x(3)
        weigh_x(1)
        nc.vector.tensor_tensor(
            g_in[0][:], g_turned[0][:].rearrange("p i n -> p n i"),
            g_factor[:].unsqueeze(1).to_broadcast([P, P, PACK]), ALU.mult,
        )
        for i in range(PACK):
            nc.scalar.activation(g_in[1][:, :, i], g_turned[1][:, i, :], ACT.Copy, scale=g_factor[:, i : i + 1])
        for c in range(2):
            quantise(u_codes[c], u_plane[c], u_in[c], E4M3)
        for h in range(2):
            quantise(g_codes[h], g_plane[h], g_in[h], E5M2)
        for c in range(2, PACK):
            weigh_x(c)
        for c in range(2, PACK):
            quantise(u_codes[c], u_plane[c], u_in[c], E4M3)
        w_bank = [ps.tile([P, PACK, P], F32, name="w_bank%d" % h, tag="w_bank%d" % h) for h in range(2)]
        for c in range(PACK):
            moment(c)

        w_in = tiles("w_in", 2, [P, P, PACK], BF16)
        w_codes = tiles("w_codes", 2, [P, P], U32)
        w_plane = tiles("w_plane", 2, [P, P], U8)
        nc.vector.tensor_copy(w_in[0][:], w_bank[0][:].rearrange("p c n -> p n c"))
        nc.scalar.copy(w_in[1][:], w_bank[1][:].rearrange("p c n -> p n c"))
        for h in (1, 0):
            quantise(w_codes[h], w_plane[h], w_in[h], E5M2)
        v_rows = tiles("v_rows", 2, [P, N], F32)
        for r in range(2):
            for h in (1, 0):
                v_bank = ps.tile([P, P], F32, name="v_bank%d_%d" % (r, h), tag="x_turned%d" % (2 * r + h))
                nc.tensor.matmul_mx(
                    out=v_bank[:],
                    lhsT=dr_codes[:, r * P : (r + 1) * P].bitcast(E4M3), lhsT_scale=dr_plane[:, r * P : (r + 1) * P],
                    rhs=w_codes[h][:].bitcast(E5M2), rhs_scale=w_plane[h][:], start=True, stop=True,
                )
                nc.scalar.copy(v_rows[r][:, h * P : (h + 1) * P], v_bank[:])
        nc.vector.tensor_copy(placed[0][:].indirect(q_list[:]), v_rows[0][:])
        nc.scalar.activation(placed[1][:].indirect(q_list[:]), v_rows[1][:], ACT.Copy)
        for r in range(2):
            edges = (0, 512, 1024) if r == 0 else (0, 512, 896, 1024)
            for q0, q1 in zip(edges, edges[1:]):
                cols = slice(q0, q1)
                result = sb.tile([P, q1 - q0], F32, name="result%d_%d" % (r, q0))
                nc.vector.scalar_tensor_tensor(result[:], placed[r][:, cols], 0.05, old_rows[r][:, cols], ALU.mult, ALU.add)
                nc.sync.dma_start(out[r * P : (r + 1) * P, cols], result[:])
